import numpy as np
import ml_dtypes


def mxq(x, axis, fmt="e4m3"):
    dtype, down = {"e4m3": (ml_dtypes.float8_e4m3fn, 7), "e5m2": (ml_dtypes.float8_e5m2, 14)}[fmt]
    v = np.moveaxis(np.asarray(x, np.float32).astype(ml_dtypes.bfloat16).astype(np.float64), axis, -1)
    blocks = v.reshape(v.shape[:-1] + (-1, 32))
    amax = np.abs(blocks).max(-1, keepdims=True)
    byte = np.maximum(np.where(amax > 0, np.frexp(amax)[1] - 1 + 127, 0) - down, 1)
    scale = np.exp2(byte - 127.0)
    codes = (blocks / scale).astype(np.float32).astype(dtype).astype(np.float64)
    return np.moveaxis((codes * scale).reshape(v.shape), -1, axis)


WIDE = False


def mx_kscale(k):
    if not WIDE:
        return np.ones(k)
    levels = np.array([30, -30])
    if k % 512:
        return np.exp2(np.random.permutation(np.resize(levels, k // 32))).repeat(32)
    a = np.empty((k // 512, 16))
    for p in range(k // 512):
        a[p, :8] = np.random.permutation(np.resize(levels, 8))
        for g in range(8):
            far = levels[np.abs(levels - a[p, g]) >= 10]
            a[p, g + 8] = far[np.random.randint(len(far))]
    return np.exp2(a.ravel()).repeat(32)


def f64(x):
    return np.asarray(x).astype(np.float64)


def striped(idx):
    return np.tile(np.asarray(idx).reshape(-1, 16).T, (8, 1)).astype(np.uint16)


def unstriped(offs):
    return offs[:16].T.reshape(-1).astype(np.int64)


E2M1 = np.array([0.0, 0.5, 1.0, 1.5, 2.0, 3.0, 4.0, 6.0, -0.0, -0.5, -1.0, -1.5, -2.0, -3.0, -4.0, -6.0])


def pack_weight(w, fmt):
    k, n = w.shape
    w = f64(np.asarray(w, np.float32).astype(ml_dtypes.bfloat16)).reshape(k // 32, 32, n)
    amax = np.abs(w).max(1)
    if fmt == "e4m3":
        byte = np.frexp(amax)[1] - 1 + 127 - 7
    else:
        mant, ex = np.frexp(amax / 6.0)
        byte = np.where(mant > 0.5, ex, ex - 1) + 127
    byte = np.clip(np.where(amax > 0, byte, 1), 1, 254)
    scaled = (w * np.exp2(127.0 - byte)[:, None, :]).reshape(k, n).astype(np.float32)
    by_word = np.ascontiguousarray(scaled.reshape(k // 512, 128, 4, n).transpose(0, 1, 3, 2))
    if fmt == "e4m3":
        words = by_word.astype(ml_dtypes.float8_e4m3fn).view(np.uint8)
    else:
        c = by_word.astype(ml_dtypes.float4_e2m1fn).view(np.uint8) & 0xF
        words = (c[..., 0::2] | (c[..., 1::2] << 4)).reshape(k // 512, 128, 2 * n)
    return np.ascontiguousarray(words), np.ascontiguousarray(byte.astype(np.uint8).reshape(k // 512, 16, n))


def unpack_weight(words, scales, fmt):
    g, _, n = scales.shape
    words = np.ascontiguousarray(words).reshape(g, 128, n, -1)
    if fmt == "e4m3":
        vals = words.view(ml_dtypes.float8_e4m3fn).astype(np.float64)
    else:
        nib = np.empty((g, 128, n, 4), np.uint8)
        nib[..., 0::2] = words & 0xF
        nib[..., 1::2] = words >> 4
        vals = E2M1[nib]
    vals = vals * np.repeat(np.exp2(scales.astype(np.float64) - 127.0), 8, axis=1)[..., None]
    return vals.transpose(0, 1, 3, 2).reshape(g * 512, n)


N, M, V, J, I, K = 512, 512, 1024, 512, 512, 512


def setup_inputs():
    n = np.random.standard_normal
    idx = np.random.permutation(V)[:J]
    idx2 = np.random.permutation(V)[:I]
    fn = mx_kscale(N)
    fm = mx_kscale(M)
    gap = pack_weight(n((N, J)) / fn[:, None], "e4m3")
    wap = pack_weight(n((N, K)) * 1 / np.sqrt(N) * fn[:, None], "e2m1")
    wbp = pack_weight(n((M, K)) * 1 / np.sqrt(M) * fm[:, None], "e4m3")
    return {
        "ga_words": gap[0],
        "ga_scales": gap[1],
        "wa_words": wap[0],
        "wa_scales": wap[1],
        "gb": (n((M, I)) / fm[:, None]).astype(np.float32),
        "wb_words": wbp[0],
        "wb_scales": wbp[1],
        "old": (0.5 * n((K, V))).astype(np.float32),
        "offs": striped(idx),
        "offs2": striped(idx2),
    }


def reference(ga_words, ga_scales, wa_words, wa_scales, gb, wb_words, wb_scales, old, offs, offs2):
    idx = unstriped(offs)
    idx2 = unstriped(offs2)
    gau = unpack_weight(ga_words, ga_scales, "e4m3")
    wau = unpack_weight(wa_words, wa_scales, "e2m1")
    wbu = unpack_weight(wb_words, wb_scales, "e4m3")
    p = wau.T @ gau
    gbq = mxq(f64(gb), 0, "e5m2")
    q = wbu.T @ gbq
    pg = np.zeros((K, V))
    pg[:, idx] = p
    qg = np.zeros((K, V))
    qg[:, idx2] = q
    y = pg + qg + 0.9 * f64(old)
    return y

from contextlib import ExitStack

import concourse.mybir as mybir

N, M, V, J, I, K = 512, 512, 1024, 512, 512, 512
FLOPS = 2 * N * K * J + 2 * M * K * I

F32 = mybir.dt.float32
BF16 = mybir.dt.bfloat16
I32 = mybir.dt.int32
U32 = mybir.dt.uint32
U16 = mybir.dt.uint16
U8 = mybir.dt.uint8
E4M3 = mybir.dt.float8_e4m3fn_x4
E5M2 = mybir.dt.float8_e5m2_x4
E2M1 = mybir.dt.float4_e2m1fn_x4
ADD = mybir.AluOpType.add
COPY = mybir.ActivationFunctionType.Copy

P = 128
BANK = 512
BLOCKS = K // P
HALVES = V // BANK
HEAD = 128
DECAY = 0.9


def tile_list_shared_table_grad_kernel(tc, ga_words, ga_scales, wa_words, wa_scales, gb, wb_words, wb_scales,
                                         old, offs, offs2, out):
    nc = tc.nc
    with ExitStack() as ctx:
        keep = ctx.enter_context(tc.tile_pool(name="keep", bufs=1))
        psum = ctx.enter_context(tc.psum_pool(name="psum", bufs=1))

        def sb(name, shape, dtype):
            return keep.tile(shape, dtype, name=name, align_bytes=64)

        list_p = keep.tile([P, J // 16], U16, name="list_p")
        list_q = keep.tile([P, I // 16], U16, name="list_q")
        ga_w = sb("ga_w", [P, J], U32)
        ga_s = sb("ga_s", [P, J], U8)
        wa_w = sb("wa_w", [P, 2 * K], U8)
        wa_s = sb("wa_s", [P, K], U8)
        wb_w = sb("wb_w", [P, K], U32)
        wb_s = sb("wb_s", [P, K], U8)
        gb_raw = [sb("gb_raw%d" % h, [P, 4 * (I // 2)], F32) for h in range(2)]
        gb_bf = sb("gb_bf", [P, 4 * I], BF16)
        gb_w = sb("gb_w", [P, I], U32)
        gb_s = sb("gb_s", [P, I], U8)
        old_raw = [sb("old_raw%d" % b, [P, V], F32) for b in range(BLOCKS)]
        old_dec = [sb("old_dec%d" % b, [P, V], F32) for b in range(BLOCKS)]
        partial = [sb("partial%d" % b, [P, V], F32) for b in range(2)]
        partial = [partial[min(b, 1)] for b in range(BLOCKS)]
        page_p = [sb("page_p%d" % s, [P, V], F32) for s in range(2)]
        page_q = [sb("page_q%d" % s, [P, V], F32) for s in range(2)]
        stage_p = [sb("stage_p0", [P, BANK], F32)[:], gb_raw[1][:, 0:BANK], gb_raw[1][:, BANK: 2 * BANK],
                   partial[0][:, BANK: 2 * BANK]]
        stage_q = [sb("stage_q%d" % b, [P, BANK], F32)[:] for b in range(BLOCKS)]
        result = [sb("result%d" % s, [P, BANK], F32) for s in range(BLOCKS * HALVES)]

        bank_head = psum.tile([P, BANK], F32, name="bank_head")
        bank_p = [psum.tile([P, BANK], F32, name="bank_p%d" % b) for b in range(BLOCKS)]
        bank_q = [psum.tile([P, BANK], F32, name="bank_q%d" % s) for s in range(2)]

        def load_scale_rows(plane, scales, quad):
            rows = scales[0, 4 * quad: 4 * quad + 4, :].bitcast(I32)
            nc.sync.dma_start(out=plane[32 * quad: 32 * quad + 32, :].bitcast(I32),
                              in_=rows.unsqueeze(0).to_broadcast([8, 4, K // 4]))

        for quad in range(3):
            load_scale_rows(wa_s, wa_scales, quad)
            load_scale_rows(ga_s, ga_scales, quad)
        nc.sync.dma_start(out=wa_w[:].bitcast(I32), in_=wa_words[0].bitcast(I32))
        nc.sync.dma_start(out=ga_w[:].bitcast(I32), in_=ga_words[0].rearrange("p n t -> p (n t)").bitcast(I32))
        load_scale_rows(wa_s, wa_scales, 3)
        load_scale_rows(ga_s, ga_scales, 3)
        nc.sync.dma_start(list_p[:], offs)
        gb_rows = gb.rearrange("(p t) i -> p t i", t=4)
        for h in range(2):
            nc.sync.dma_start(out=gb_raw[h][:].rearrange("p (t i) -> p t i", t=4),
                              in_=gb_rows[:, :, h * (I // 2): (h + 1) * (I // 2)])
        nc.sync.dma_start(out=wb_w[:].bitcast(I32), in_=wb_words[0].rearrange("p n t -> p (n t)").bitcast(I32))
        for quad in range(4):
            load_scale_rows(wb_s, wb_scales, quad)
        nc.sync.dma_start(list_q[:], offs2)
        for b in range(BLOCKS):
            nc.sync.dma_start(out=old_raw[b][:], in_=old[b * P: (b + 1) * P, :])

        for page in page_p + page_q:
            nc.vector.memset(page[:].bitcast(I32), 0)

        def product_p(b, dst, j0, j1):
            nc.tensor.matmul_mx(out=dst, lhsT=wa_w[:, 2 * P * b: 2 * P * (b + 1)].bitcast(E2M1),
                                lhsT_scale=wa_s[:, P * b: P * (b + 1)], rhs=ga_w[:, j0:j1].bitcast(E4M3),
                                rhs_scale=ga_s[:, j0:j1], start=True, stop=True)

        def product_q(b, dst):
            nc.tensor.matmul_mx(out=dst, lhsT=wb_w[:, P * b: P * (b + 1)].bitcast(E4M3),
                                lhsT_scale=wb_s[:, P * b: P * (b + 1)], rhs=gb_w[:].bitcast(E5M2),
                                rhs_scale=gb_s[:], start=True, stop=True)

        def scatter(page, lst, src, j0, j1):
            nc.vector.tensor_copy(page[:].indirect(lst[:, j0 // 16: j1 // 16]), src[:, j0:j1])

        def make_p(b):
            product_p(b, bank_p[b][:], 0, J)
            nc.scalar.copy(stage_p[b], bank_p[b][:])

        def make_q(b):
            product_q(b, bank_q[b % 2][:])
            nc.scalar.copy(stage_q[b], bank_q[b % 2][:])

        def put_p(b):
            scatter(page_p[b % 2], list_p, stage_p[b], 0, J)

        def put_q(b):
            scatter(page_q[b % 2], list_q, stage_q[b], 0, I)

        def decay_old(b):
            nc.scalar.activation(old_dec[b][:], old_raw[b][:], COPY, scale=DECAY)

        def add_p(b):
            nc.gpsimd.tensor_tensor(partial[b][:], page_p[b % 2][:], old_dec[b][:], ADD)

        def add_q(b, engine):
            for h in range(HALVES):
                cols = slice(h * BANK, (h + 1) * BANK)
                engine.tensor_tensor(result[HALVES * b + h][:], partial[b][:, cols], page_q[b % 2][:, cols], ADD)
                nc.sync.dma_start(out=out[b * P: (b + 1) * P, cols], in_=result[HALVES * b + h][:])

        product_p(0, bank_head[:, 0:HEAD], 0, HEAD)
        nc.scalar.copy(stage_p[0][:, 0:HEAD], bank_head[:, 0:HEAD])
        scatter(page_p[0], list_p, stage_p[0], 0, HEAD)
        product_p(0, bank_p[0][:, HEAD: 2 * HEAD], HEAD, 2 * HEAD)
        product_p(0, bank_p[0][:, 2 * HEAD: J], 2 * HEAD, J)
        nc.scalar.copy(stage_p[0][:, HEAD:J], bank_p[0][:, HEAD:J])
        scatter(page_p[0], list_p, stage_p[0], HEAD, J)

        for h in range(2):
            cols = gb_bf[:, h * 2 * I: (h + 1) * 2 * I]
            nc.scalar.copy(cols.rearrange("p (c i t) -> p c t i", i=4, t=4),
                           gb_raw[h][:].rearrange("p (t c i) -> p c t i", t=4, i=4))
        nc.vector.quantize_mx(out=gb_w[:].bitcast(E5M2), scales=gb_s[:], in_=gb_bf[:])

        make_p(1)
        put_p(1)
        make_q(0)
        put_q(0)
        make_q(1)
        put_q(1)
        decay_old(0)
        add_p(0)
        make_p(2)
        put_p(2)
        decay_old(1)
        add_p(1)
        make_q(2)
        make_q(3)
        decay_old(2)
        decay_old(3)
        add_q(0, nc.gpsimd)
        put_q(2)
        make_p(3)
        put_p(3)
        add_q(1, nc.gpsimd)
        put_q(3)
        add_p(2)
        add_q(2, nc.gpsimd)
        add_p(3)
        add_q(3, nc.vector)
